import numpy as np
import ml_dtypes

BF16 = ml_dtypes.bfloat16


def bf(x):
    return np.asarray(x, np.float32).astype(BF16)


def f32(x):
    return np.asarray(x, np.float32)


def f64(x):
    return np.asarray(x).astype(np.float64)


def striped(idx):
    return np.tile(idx.reshape(-1, 16).T, (8, 1))


def rows(idx, k):
    return np.tile(idx, (k, 1))


def look(tab, idx):
    return np.take_along_axis(f64(tab), rows(idx, len(tab)), axis=1)


K, S, V, N = 256, 2048, 512, 512


def setup_inputs():
    return {"tab": f32(np.random.standard_normal((2, K, S))), "y": f32(np.random.standard_normal((K, V))), "offs": striped(np.random.permutation(S)[:N])}


def reference(tab, y, offs):
    idx = offs[:16].T.reshape(-1)
    x = (np.maximum(look(tab[0], idx), f64(y))) * (np.maximum(look(tab[1], idx), 0.0))
    return x

@@ -1,0 +1,42 @@
+import concourse.mybir as mybir
+
+F32, U16 = mybir.dt.float32, mybir.dt.uint16
+MAX, MULT = mybir.AluOpType.max, mybir.AluOpType.mult
+RELU = mybir.ActivationFunctionType.Relu
+
+P = 128
+ROWS = 256
+PLACES = 2048
+N = 512
+BLOCKS = ROWS // P
+
+FLOPS = 3 * ROWS * N
+
+
+def tile_lookup_vg_maxrelu_out_kernel(tc, tab, y, offs, out):
+    nc = tc.nc
+    with (
+        tc.tile_pool(name="held", bufs=1) as held,
+        tc.tile_pool(name="blocks", bufs=BLOCKS) as blocks,
+    ):
+        offsets = held.tile([P, N // 16], U16, name="offsets")
+        nc.sync.dma_start(offsets[:], offs)
+
+        for b in range(BLOCKS):
+            rows = slice(b * P, (b + 1) * P)
+            values = blocks.tile([P, PLACES], F32, name="values")
+            gates = blocks.tile([P, PLACES], F32, name="gates")
+            stream = blocks.tile([P, N], F32, name="stream")
+            nc.sync.dma_start(gates[:], tab[1, rows, :])
+            nc.sync.dma_start(stream[:], y[rows, :])
+            nc.sync.dma_start(values[:], tab[0, rows, :])
+
+            gate = blocks.tile([P, N], F32, name="gate")
+            nc.scalar.activation(gate[:], gates[:].indirect(offsets[:]), RELU)
+
+            top = blocks.tile([P, N], F32, name="top")
+            nc.vector.tensor_tensor(top[:], values[:].indirect(offsets[:]), stream[:], MAX)
+
+            product = blocks.tile([P, N], F32, name="product")
+            nc.vector.tensor_tensor(product[:], top[:], gate[:], MULT)
+            nc.sync.dma_start(out[rows, :], product[:])

@@ -22,21 +22,23 @@ def tile_lookup_vg_maxrelu_out_kernel(tc, tab, y, offs, out):
         offsets = held.tile([P, N // 16], U16, name="offsets")
         nc.sync.dma_start(offsets[:], offs)
 
+        tops = []
         for b in range(BLOCKS):
             rows = slice(b * P, (b + 1) * P)
-            values = blocks.tile([P, PLACES], F32, name="values")
-            gates = blocks.tile([P, PLACES], F32, name="gates")
             stream = blocks.tile([P, N], F32, name="stream")
-            nc.sync.dma_start(gates[:], tab[1, rows, :])
             nc.sync.dma_start(stream[:], y[rows, :])
+            values = blocks.tile([P, PLACES], F32, name="values")
             nc.sync.dma_start(values[:], tab[0, rows, :])
-
-            gate = blocks.tile([P, N], F32, name="gate")
-            nc.scalar.activation(gate[:], gates[:].indirect(offsets[:]), RELU)
-
             top = blocks.tile([P, N], F32, name="top")
             nc.vector.tensor_tensor(top[:], values[:].indirect(offsets[:]), stream[:], MAX)
+            tops.append(top)
 
+        for b in range(BLOCKS):
+            rows = slice(b * P, (b + 1) * P)
+            gates = blocks.tile([P, PLACES], F32, name="gates")
+            nc.sync.dma_start(gates[:], tab[1, rows, :])
+            gate = blocks.tile([P, N], F32, name="gate")
+            nc.scalar.activation(gate[:], gates[:].indirect(offsets[:]), RELU)
             product = blocks.tile([P, N], F32, name="product")
-            nc.vector.tensor_tensor(product[:], top[:], gate[:], MULT)
+            nc.vector.tensor_tensor(product[:], tops[b][:], gate[:], MULT)
             nc.sync.dma_start(out[rows, :], product[:])

@@ -9,6 +9,9 @@ ROWS = 256
 PLACES = 2048
 N = 512
 BLOCKS = ROWS // P
+PIECES = 2
+PIECE = N // PIECES
+COLS = PIECE // 16
 
 FLOPS = 3 * ROWS * N
 
@@ -21,6 +24,11 @@ def tile_lookup_vg_maxrelu_out_kernel(tc, tab, y, offs, out):
     ):
         offsets = held.tile([P, N // 16], U16, name="offsets")
         nc.sync.dma_start(offsets[:], offs)
+
+        zeros = held.tile([P, 1], F32, name="zeros")
+        warmed = held.tile([P, 1], F32, name="warmed")
+        nc.vector.memset(zeros[:], 0.0)
+        nc.scalar.activation(warmed[:], zeros[:], RELU)
 
         tops = []
         for b in range(BLOCKS):
@@ -38,7 +46,12 @@ def tile_lookup_vg_maxrelu_out_kernel(tc, tab, y, offs, out):
             gates = blocks.tile([P, PLACES], F32, name="gates")
             nc.sync.dma_start(gates[:], tab[1, rows, :])
             gate = blocks.tile([P, N], F32, name="gate")
-            nc.scalar.activation(gate[:], gates[:].indirect(offsets[:]), RELU)
+            top = tops[b]
             product = blocks.tile([P, N], F32, name="product")
-            nc.vector.tensor_tensor(product[:], tops[b][:], gate[:], MULT)
-            nc.sync.dma_start(out[rows, :], product[:])
+            for k in range(PIECES):
+                piece = slice(k * PIECE, (k + 1) * PIECE)
+                nc.scalar.activation(
+                    gate[:, piece], gates[:].indirect(offsets[:, k * COLS : (k + 1) * COLS]), RELU
+                )
+                nc.vector.tensor_tensor(product[:, piece], top[:, piece], gate[:, piece], MULT)
+                nc.sync.dma_start(out[rows, piece], product[:, piece])

@@ -9,7 +9,7 @@ ROWS = 256
 PLACES = 2048
 N = 512
 BLOCKS = ROWS // P
-PIECES = 2
+PIECES = 4
 PIECE = N // PIECES
 COLS = PIECE // 16
 

import concourse.mybir as mybir

F32, U16 = mybir.dt.float32, mybir.dt.uint16
MAX, MULT = mybir.AluOpType.max, mybir.AluOpType.mult
RELU = mybir.ActivationFunctionType.Relu

P = 128
ROWS = 256
PLACES = 2048
N = 512
BLOCKS = ROWS // P
PIECES = 4
PIECE = N // PIECES
COLS = PIECE // 16

FLOPS = 3 * ROWS * N


def tile_lookup_vg_maxrelu_out_kernel(tc, tab, y, offs, out):
    nc = tc.nc
    with (
        tc.tile_pool(name="held", bufs=1) as held,
        tc.tile_pool(name="blocks", bufs=BLOCKS) as blocks,
    ):
        offsets = held.tile([P, N // 16], U16, name="offsets")
        nc.sync.dma_start(offsets[:], offs)

        zeros = held.tile([P, 1], F32, name="zeros")
        warmed = held.tile([P, 1], F32, name="warmed")
        nc.vector.memset(zeros[:], 0.0)
        nc.scalar.activation(warmed[:], zeros[:], RELU)

        tops = []
        for b in range(BLOCKS):
            rows = slice(b * P, (b + 1) * P)
            stream = blocks.tile([P, N], F32, name="stream")
            nc.sync.dma_start(stream[:], y[rows, :])
            values = blocks.tile([P, PLACES], F32, name="values")
            nc.sync.dma_start(values[:], tab[0, rows, :])
            top = blocks.tile([P, N], F32, name="top")
            nc.vector.tensor_tensor(top[:], values[:].indirect(offsets[:]), stream[:], MAX)
            tops.append(top)

        for b in range(BLOCKS):
            rows = slice(b * P, (b + 1) * P)
            gates = blocks.tile([P, PLACES], F32, name="gates")
            nc.sync.dma_start(gates[:], tab[1, rows, :])
            gate = blocks.tile([P, N], F32, name="gate")
            top = tops[b]
            product = blocks.tile([P, N], F32, name="product")
            for k in range(PIECES):
                piece = slice(k * PIECE, (k + 1) * PIECE)
                nc.scalar.activation(
                    gate[:, piece], gates[:].indirect(offsets[:, k * COLS : (k + 1) * COLS]), RELU
                )
                nc.vector.tensor_tensor(product[:, piece], top[:, piece], gate[:, piece], MULT)
                nc.sync.dma_start(out[rows, piece], product[:, piece])
